import numpy as np
import ml_dtypes


def mxq(x, axis, fmt="e4m3"):
    dtype, down = {"e4m3": (ml_dtypes.float8_e4m3fn, 7), "e5m2": (ml_dtypes.float8_e5m2, 14)}[fmt]
    v = np.moveaxis(np.asarray(x, np.float32).astype(ml_dtypes.bfloat16).astype(np.float64), axis, -1)
    blocks = v.reshape(v.shape[:-1] + (-1, 32))
    amax = np.abs(blocks).max(-1, keepdims=True)
    byte = np.maximum(np.where(amax > 0, np.frexp(amax)[1] - 1 + 127, 0) - down, 1)
    scale = np.exp2(byte - 127.0)
    codes = (blocks / scale).astype(np.float32).astype(dtype).astype(np.float64)
    return np.moveaxis((codes * scale).reshape(v.shape), -1, axis)


WIDE = False


def mx_kscale(k):
    if not WIDE:
        return np.ones(k)
    levels = np.array([10, -10, 5, -5, 0])
    if k % 512:
        return np.exp2(np.random.permutation(np.resize(levels, k // 32))).repeat(32)
    a = np.empty((k // 512, 16))
    for p in range(k // 512):
        a[p, :8] = np.random.permutation(np.resize(levels, 8))
        for g in range(8):
            far = levels[np.abs(levels - a[p, g]) >= 10]
            a[p, g + 8] = far[np.random.randint(len(far))]
    return np.exp2(a.ravel()).repeat(32)


def f64(x):
    return np.asarray(x).astype(np.float64)


def striped(idx):
    return np.tile(np.asarray(idx).reshape(-1, 16).T, (8, 1)).astype(np.uint16)


def unstriped(offs):
    return offs[:16].T.reshape(-1).astype(np.int64)


E2M1 = np.array([0.0, 0.5, 1.0, 1.5, 2.0, 3.0, 4.0, 6.0, -0.0, -0.5, -1.0, -1.5, -2.0, -3.0, -4.0, -6.0])


def pack_weight(w, fmt):
    k, n = w.shape
    w = f64(np.asarray(w, np.float32).astype(ml_dtypes.bfloat16)).reshape(k // 32, 32, n)
    amax = np.abs(w).max(1)
    if fmt == "e4m3":
        byte = np.frexp(amax)[1] - 1 + 127 - 7
    else:
        mant, ex = np.frexp(amax / 6.0)
        byte = np.where(mant > 0.5, ex, ex - 1) + 127
    byte = np.clip(np.where(amax > 0, byte, 1), 1, 254)
    scaled = (w * np.exp2(127.0 - byte)[:, None, :]).reshape(k, n).astype(np.float32)
    by_word = np.ascontiguousarray(scaled.reshape(k // 512, 128, 4, n).transpose(0, 1, 3, 2))
    if fmt == "e4m3":
        words = by_word.astype(ml_dtypes.float8_e4m3fn).view(np.uint8)
    else:
        c = by_word.astype(ml_dtypes.float4_e2m1fn).view(np.uint8) & 0xF
        words = (c[..., 0::2] | (c[..., 1::2] << 4)).reshape(k // 512, 128, 2 * n)
    return np.ascontiguousarray(words), np.ascontiguousarray(byte.astype(np.uint8).reshape(k // 512, 16, n))


def unpack_weight(words, scales, fmt):
    g, _, n = scales.shape
    words = np.ascontiguousarray(words).reshape(g, 128, n, -1)
    if fmt == "e4m3":
        vals = words.view(ml_dtypes.float8_e4m3fn).astype(np.float64)
    else:
        nib = np.empty((g, 128, n, 4), np.uint8)
        nib[..., 0::2] = words & 0xF
        nib[..., 1::2] = words >> 4
        vals = E2M1[nib]
    vals = vals * np.repeat(np.exp2(scales.astype(np.float64) - 127.0), 8, axis=1)[..., None]
    return vals.transpose(0, 1, 3, 2).reshape(g * 512, n)


def bf(x):
    return np.asarray(x, np.float32).astype(ml_dtypes.bfloat16)


def planes(Y):
    r, m = Y.shape
    b = f64(bf(Y)).reshape(r // 32, 32, m)
    amax = np.abs(b).max(1)
    byte = np.clip(np.where(amax > 0, np.frexp(amax)[1] - 1 + 127 - 7, 1), 1, 254)
    codes = (b * np.exp2(127.0 - byte)[:, None, :]).reshape(r, m).astype(np.float32).astype(ml_dtypes.float8_e4m3fn).view(np.uint8)
    words = codes.reshape(r // 512, 128, 4, m).transpose(0, 1, 3, 2)
    return np.ascontiguousarray(words), np.ascontiguousarray(byte.astype(np.uint8).reshape(r // 512, 16, m))


D, T, I, J, U, M, N = 512, 2048, 512, 512, 1024, 512, 64


def setup_inputs():
    n = np.random.standard_normal
    idx = np.random.permutation(T)[:I]
    idx2 = np.random.permutation(U)[:J]
    idx3 = np.random.permutation(U)[:J]
    idx4 = np.random.permutation(M)[:N]
    fd = mx_kscale(D)
    keysp = pack_weight(n((D, T)) / fd[:, None], "e2m1")
    return {
        "keys_words": keysp[0],
        "keys_scales": keysp[1],
        "notes": (n((D, U)) * 1.0 / np.sqrt(D) * fd[:, None]).astype(np.float32),
        "old": (1.0 * n((I, M))).astype(np.float32),
        "offs": striped(idx),
        "offs2": striped(idx2),
        "offs3": striped(idx3),
        "offs4": striped(idx4),
    }


def reference(keys_words, keys_scales, notes, old, offs, offs2, offs3, offs4):
    idx = unstriped(offs)
    idx2 = unstriped(offs2)
    idx3 = unstriped(offs3)
    idx4 = unstriped(offs4)
    keysu = unpack_weight(keys_words, keys_scales, "e2m1")
    keysidxg = keysu[:, idx]
    notesq = mxq(f64(notes), 0, "e4m3")
    g1 = keysidxg.T @ notesq
    g0 = g1[:, idx2] - g1[:, idx3]
    rb0 = g0.reshape(I, N, J // N).max(axis=2)
    gf = np.zeros((I, M))
    gf[:, idx4] = rb0
    y = f64(old) + gf
    words, scales = planes(y)
    return y, words, scales

@@ -1,0 +1,165 @@
+from contextlib import ExitStack
+
+import concourse.mybir as mybir
+
+D, T, I, J, U, M, RUNS = 512, 2048, 512, 512, 1024, 512, 64
+RUN = J // RUNS
+FLOPS = 2 * D * I * U
+
+F32 = mybir.dt.float32
+BF16 = mybir.dt.bfloat16
+I32 = mybir.dt.int32
+U32 = mybir.dt.uint32
+U16 = mybir.dt.uint16
+U8 = mybir.dt.uint8
+FP8X4 = mybir.dt.float8_e4m3fn_x4
+FP4X4 = mybir.dt.float4_e2m1fn_x4
+COPY = mybir.ActivationFunctionType.Copy
+ALU = mybir.AluOpType
+
+P = 128
+PACK = 4
+BANK = 512
+CHUNK = 256
+
+
+def tile_attend_tab_looked_runsput_pl_kernel(
+    tc, keys_words, keys_scales, notes, old, offs, offs2, offs3, offs4, out_0, out_1, out_2
+):
+    nc = tc.nc
+    with ExitStack() as ctx:
+        sb = ctx.enter_context(tc.tile_pool(name="sb", bufs=1))
+        ps = ctx.enter_context(tc.psum_pool(name="ps", bufs=1))
+
+        key_list = sb.tile([P, I // 16], U16, name="key_list")
+        plus_list = sb.tile([P, J // 16], U16, name="plus_list")
+        minus_list = sb.tile([P, J // 16], U16, name="minus_list")
+        put_list = sb.tile([P, RUNS // 16], U16, name="put_list")
+
+        pool_words = sb.tile([P, T], U16, name="pool_words", align_bytes=64)
+        pool_scales = sb.tile([P, T], U8, name="pool_scales", align_bytes=64)
+        nc.gpsimd.memset(pool_scales[:].bitcast(I32), 0)
+        nc.sync.dma_start(key_list[:], offs)
+        nc.sync.dma_start(pool_words[:].bitcast(I32), keys_words[0].bitcast(I32))
+        for q in range(4):
+            nc.scalar.dma_start(
+                pool_scales[32 * q : 32 * q + 4, :].bitcast(I32),
+                keys_scales[0, 4 * q : 4 * q + 4, :].bitcast(I32),
+            )
+
+        notes_v = notes.rearrange("(p t) u -> p t u", t=PACK)
+        nchunks = U // CHUNK
+        raw = []
+        for c in range(nchunks):
+            tile = sb.tile([P, PACK, CHUNK], F32, name="raw%d" % c)
+            nc.sync.dma_start(tile[:], notes_v[:, :, c * CHUNK : (c + 1) * CHUNK])
+            raw.append(tile)
+        nc.sync.dma_start(minus_list[:], offs3)
+        nc.sync.dma_start(plus_list[:], offs2)
+        nc.sync.dma_start(put_list[:], offs4)
+        old_sb = sb.tile([P, PACK, M], F32, name="old_sb")
+        nc.sync.dma_start(old_sb[:], old.rearrange("(p r) m -> p r m", r=PACK))
+
+        put = []
+        for r in range(PACK):
+            tile = sb.tile([P, M], F32, name="put%d" % r)
+            nc.gpsimd.memset(tile[:], 0.0)
+            put.append(tile)
+
+        picked_words = sb.tile([P, I], U16, name="picked_words", align_bytes=64)
+        key_words = sb.tile([P, 2 * I], U8, name="key_words", align_bytes=64)
+        key_scales = sb.tile([P, I], U8, name="key_scales", align_bytes=64)
+        nc.vector.tensor_copy(picked_words[:], pool_words[:].indirect(key_list[:]))
+        nc.vector.tensor_copy(
+            key_words[:].bitcast(U16).rearrange("p (r s) -> p r s", r=PACK),
+            picked_words[:].rearrange("p (s r) -> p r s", r=PACK),
+        )
+        nc.vector.tensor_copy(
+            key_scales[:].rearrange("p (r s) -> p s r", r=PACK),
+            pool_scales[:].indirect(key_list[:]),
+        )
+
+        banks = [
+            [ps.tile([P, BANK], F32, name="bank%d_%d" % (r, h)) for h in range(U // BANK)]
+            for r in range(PACK)
+        ]
+        g1 = [sb.tile([P, U], F32, name="g1_%d" % r) for r in range(PACK)]
+
+        def multiply(c, codes, scales):
+            h, col = divmod(c * CHUNK, BANK)
+            for r in range(PACK):
+                nc.tensor.matmul_mx(
+                    out=banks[r][h][:, col : col + CHUNK],
+                    lhsT=key_words[:, 2 * P * r : 2 * P * (r + 1)].bitcast(FP4X4),
+                    lhsT_scale=key_scales[:, P * r : P * (r + 1)],
+                    rhs=codes[:].bitcast(FP8X4),
+                    rhs_scale=scales[:],
+                    start=True,
+                    stop=True,
+                )
+
+        for c in range(nchunks):
+            woven = sb.tile([P, CHUNK, PACK], BF16, name="woven%d" % c, align_bytes=64)
+            src = raw[c][:].rearrange("p t (g i) -> p g t i", i=4)
+            dst = woven[:].rearrange("p (g i) t -> p g t i", i=4)
+            if c < 2:
+                nc.scalar.activation(dst, src, COPY)
+            else:
+                nc.vector.tensor_copy(dst, src)
+            codes = sb.tile([P, CHUNK], U32, name="codes%d" % c, align_bytes=64)
+            scales = sb.tile([P, CHUNK], U8, name="scales%d" % c, align_bytes=64)
+            nc.vector.quantize_mx(
+                out=codes[:].bitcast(FP8X4),
+                scales=scales[:],
+                in_=woven[:].rearrange("p u t -> p (u t)"),
+            )
+            multiply(c, codes, scales)
+            if c == 1:
+                for r in range(PACK):
+                    nc.scalar.activation(g1[r][:, 0:BANK], banks[r][0][:], COPY)
+
+        y = sb.tile([P, PACK, M], F32, name="y")
+        out_v = out_0.rearrange("(p r) m -> p r m", r=PACK)
+        for r in range(PACK):
+            if r < 3:
+                nc.vector.tensor_copy(g1[r][:, BANK:U], banks[r][1][:])
+            else:
+                nc.scalar.activation(g1[r][:, BANK:U], banks[r][1][:], COPY)
+        for r in range(PACK):
+            minus = sb.tile([P, J], F32, name="minus%d" % r)
+            nc.scalar.activation(minus[:], g1[r][:].indirect(minus_list[:]), COPY)
+            g0 = sb.tile([P, J], F32, name="g0_%d" % r)
+            nc.vector.tensor_tensor(g0[:], g1[r][:].indirect(plus_list[:]), minus[:], ALU.subtract)
+            top = sb.tile([P, RUNS], F32, name="top%d" % r)
+            nc.vector.tensor_reduce(
+                top[:], g0[:].rearrange("p (n j) -> p n j", j=RUN), mybir.AxisListType.X, ALU.max
+            )
+            nc.scalar.activation(put[r][:].indirect(put_list[:]), top[:], COPY)
+            nc.vector.tensor_tensor(y[:, r, :], old_sb[:, r, :], put[r][:], ALU.add)
+            nc.sync.dma_start(out_v[:, r, :], y[:, r, :])
+
+        y_scales = sb.tile([P, M], U8, name="y_scales", align_bytes=64)
+        words_v = out_1[0].rearrange("p m t -> p (m t)").bitcast(I32)
+        half = M // 2
+        for h in range(2):
+            cols = slice(h * half, (h + 1) * half)
+            y_woven = sb.tile([P, half, PACK], BF16, name="y_woven%d" % h, align_bytes=64)
+            src = y[:, :, cols].rearrange("p r (g i) -> p g r i", i=4)
+            dst = y_woven[:].rearrange("p (g i) r -> p g r i", i=4)
+            if h == 0:
+                nc.vector.tensor_copy(dst, src)
+            else:
+                nc.scalar.activation(dst, src, COPY)
+            y_codes = sb.tile([P, half], U32, name="y_codes%d" % h, align_bytes=64)
+            nc.vector.quantize_mx(
+                out=y_codes[:].bitcast(FP8X4),
+                scales=y_scales[:, cols],
+                in_=y_woven[:].rearrange("p m r -> p (m r)"),
+            )
+            nc.sync.dma_start(words_v[:, cols], y_codes[:].bitcast(I32))
+        for q in range(4):
+            queue = nc.sync if q % 2 == 0 else nc.scalar
+            queue.dma_start(
+                out_2[0, 4 * q : 4 * q + 4, :].bitcast(I32),
+                y_scales[32 * q : 32 * q + 4, :].bitcast(I32),
+            )

@@ -20,7 +20,8 @@ ALU = mybir.AluOpType
 P = 128
 PACK = 4
 BANK = 512
-CHUNK = 256
+WIDTHS = [256, 256, 128, 256, 128]
+STARTS = [sum(WIDTHS[:c]) for c in range(len(WIDTHS))]
 
 
 def tile_attend_tab_looked_runsput_pl_kernel(
@@ -39,21 +40,21 @@ def tile_attend_tab_looked_runsput_pl_kernel(
         pool_words = sb.tile([P, T], U16, name="pool_words", align_bytes=64)
         pool_scales = sb.tile([P, T], U8, name="pool_scales", align_bytes=64)
         nc.gpsimd.memset(pool_scales[:].bitcast(I32), 0)
-        nc.sync.dma_start(key_list[:], offs)
         nc.sync.dma_start(pool_words[:].bitcast(I32), keys_words[0].bitcast(I32))
-        for q in range(4):
-            nc.scalar.dma_start(
-                pool_scales[32 * q : 32 * q + 4, :].bitcast(I32),
-                keys_scales[0, 4 * q : 4 * q + 4, :].bitcast(I32),
-            )
+        nc.sync.dma_start(key_list[:], offs)
 
         notes_v = notes.rearrange("(p t) u -> p t u", t=PACK)
-        nchunks = U // CHUNK
         raw = []
-        for c in range(nchunks):
-            tile = sb.tile([P, PACK, CHUNK], F32, name="raw%d" % c)
-            nc.sync.dma_start(tile[:], notes_v[:, :, c * CHUNK : (c + 1) * CHUNK])
+        for c, width in enumerate(WIDTHS):
+            tile = sb.tile([P, PACK, width], F32, name="raw%d" % c)
+            nc.sync.dma_start(tile[:], notes_v[:, :, STARTS[c] : STARTS[c] + width])
             raw.append(tile)
+            if c == 0:
+                for q in range(4):
+                    nc.sync.dma_start(
+                        pool_scales[32 * q : 32 * q + 4, :].bitcast(I32),
+                        keys_scales[0, 4 * q : 4 * q + 4, :].bitcast(I32),
+                    )
         nc.sync.dma_start(minus_list[:], offs3)
         nc.sync.dma_start(plus_list[:], offs2)
         nc.sync.dma_start(put_list[:], offs4)
@@ -63,7 +64,8 @@ def tile_attend_tab_looked_runsput_pl_kernel(
         put = []
         for r in range(PACK):
             tile = sb.tile([P, M], F32, name="put%d" % r)
-            nc.gpsimd.memset(tile[:], 0.0)
+            engine = nc.gpsimd if r < 2 else nc.vector
+            engine.memset(tile[:], 0.0)
             put.append(tile)
 
         picked_words = sb.tile([P, I], U16, name="picked_words", align_bytes=64)
@@ -79,86 +81,158 @@ def tile_attend_tab_looked_runsput_pl_kernel(
             pool_scales[:].indirect(key_list[:]),
         )
 
-        banks = [
-            [ps.tile([P, BANK], F32, name="bank%d_%d" % (r, h)) for h in range(U // BANK)]
-            for r in range(PACK)
-        ]
+        def move(on_vector, dst, src):
+            if on_vector:
+                nc.vector.tensor_copy(dst, src)
+            else:
+                nc.scalar.copy(dst, src)
+
+        woven, note_codes, note_scales = {}, {}, {}
+
+        def weave(c):
+            woven[c] = sb.tile([P, WIDTHS[c], PACK], BF16, name="woven%d" % c, align_bytes=64)
+            dst = woven[c][:].rearrange("p (g i) t -> p g t i", i=4)
+            src = raw[c][:].rearrange("p t (g i) -> p g t i", i=4)
+            if c == 0:
+                nc.scalar.activation(dst, src, COPY)
+            else:
+                move(c >= 3, dst, src)
+
+        def quantise(c):
+            note_codes[c] = sb.tile([P, WIDTHS[c]], U32, name="codes%d" % c, align_bytes=64)
+            note_scales[c] = sb.tile([P, WIDTHS[c]], U8, name="scales%d" % c, align_bytes=64)
+            nc.vector.quantize_mx(
+                out=note_codes[c][:].bitcast(FP8X4),
+                scales=note_scales[c][:],
+                in_=woven[c][:].rearrange("p u t -> p (u t)"),
+            )
+
+        weave(0)
+        for c in range(1, len(WIDTHS)):
+            weave(c)
+            quantise(c - 1)
+        quantise(len(WIDTHS) - 1)
+
+        groups = [((0, 1), "a"), ((2, 3), "b"), ((4,), "a")]
         g1 = [sb.tile([P, U], F32, name="g1_%d" % r) for r in range(PACK)]
 
-        def multiply(c, codes, scales):
-            h, col = divmod(c * CHUNK, BANK)
-            for r in range(PACK):
+        def product(r, g, on_vector):
+            chunks, tag = groups[g]
+            start = STARTS[chunks[0]]
+            span = sum(WIDTHS[c] for c in chunks)
+            owner = 0 if (r, g) == (PACK - 1, 0) else r
+            bank = ps.tile([P, span], F32, name="bank", tag="%s%d" % (tag, owner))
+            for c in chunks:
+                col = STARTS[c] - start
                 nc.tensor.matmul_mx(
-                    out=banks[r][h][:, col : col + CHUNK],
+                    out=bank[:, col : col + WIDTHS[c]],
                     lhsT=key_words[:, 2 * P * r : 2 * P * (r + 1)].bitcast(FP4X4),
                     lhsT_scale=key_scales[:, P * r : P * (r + 1)],
-                    rhs=codes[:].bitcast(FP8X4),
-                    rhs_scale=scales[:],
+                    rhs=note_codes[c][:].bitcast(FP8X4),
+                    rhs_scale=note_scales[c][:],
                     start=True,
                     stop=True,
                 )
-
-        for c in range(nchunks):
-            woven = sb.tile([P, CHUNK, PACK], BF16, name="woven%d" % c, align_bytes=64)
-            src = raw[c][:].rearrange("p t (g i) -> p g t i", i=4)
-            dst = woven[:].rearrange("p (g i) t -> p g t i", i=4)
-            if c < 2:
-                nc.scalar.activation(dst, src, COPY)
-            else:
-                nc.vector.tensor_copy(dst, src)
-            codes = sb.tile([P, CHUNK], U32, name="codes%d" % c, align_bytes=64)
-            scales = sb.tile([P, CHUNK], U8, name="scales%d" % c, align_bytes=64)
-            nc.vector.quantize_mx(
-                out=codes[:].bitcast(FP8X4),
-                scales=scales[:],
-                in_=woven[:].rearrange("p u t -> p (u t)"),
-            )
-            multiply(c, codes, scales)
-            if c == 1:
-                for r in range(PACK):
-                    nc.scalar.activation(g1[r][:, 0:BANK], banks[r][0][:], COPY)
+            move(on_vector, g1[r][:, start : start + span], bank[:])
 
         y = sb.tile([P, PACK, M], F32, name="y")
         out_v = out_0.rearrange("(p r) m -> p r m", r=PACK)
-        for r in range(PACK):
-            if r < 3:
-                nc.vector.tensor_copy(g1[r][:, BANK:U], banks[r][1][:])
-            else:
-                nc.scalar.activation(g1[r][:, BANK:U], banks[r][1][:], COPY)
-        for r in range(PACK):
-            minus = sb.tile([P, J], F32, name="minus%d" % r)
-            nc.scalar.activation(minus[:], g1[r][:].indirect(minus_list[:]), COPY)
-            g0 = sb.tile([P, J], F32, name="g0_%d" % r)
-            nc.vector.tensor_tensor(g0[:], g1[r][:].indirect(plus_list[:]), minus[:], ALU.subtract)
-            top = sb.tile([P, RUNS], F32, name="top%d" % r)
-            nc.vector.tensor_reduce(
-                top[:], g0[:].rearrange("p (n j) -> p n j", j=RUN), mybir.AxisListType.X, ALU.max
-            )
-            nc.scalar.activation(put[r][:].indirect(put_list[:]), top[:], COPY)
-            nc.vector.tensor_tensor(y[:, r, :], old_sb[:, r, :], put[r][:], ALU.add)
+        half = M // 2
+
+        def add_old(r, cols):
+            nc.vector.tensor_tensor(y[:, r, cols], old_sb[:, r, cols], put[r][:, cols], ALU.add)
+
+        def store(r):
             nc.sync.dma_start(out_v[:, r, :], y[:, r, :])
 
-        y_scales = sb.tile([P, M], U8, name="y_scales", align_bytes=64)
-        words_v = out_1[0].rearrange("p m t -> p (m t)").bitcast(I32)
-        half = M // 2
-        for h in range(2):
-            cols = slice(h * half, (h + 1) * half)
-            y_woven = sb.tile([P, half, PACK], BF16, name="y_woven%d" % h, align_bytes=64)
-            src = y[:, :, cols].rearrange("p r (g i) -> p g r i", i=4)
-            dst = y_woven[:].rearrange("p (g i) r -> p g r i", i=4)
-            if h == 0:
-                nc.vector.tensor_copy(dst, src)
-            else:
-                nc.scalar.activation(dst, src, COPY)
-            y_codes = sb.tile([P, half], U32, name="y_codes%d" % h, align_bytes=64)
-            nc.vector.quantize_mx(
-                out=y_codes[:].bitcast(FP8X4),
-                scales=y_scales[:, cols],
-                in_=y_woven[:].rearrange("p m r -> p (m r)"),
+        whole, left, right = slice(0, M), slice(0, half), slice(half, M)
+
+        minus, g0 = {}, {}
+
+        def look_up(r, name, offsets):
+            tile = sb.tile([P, J], F32, name="%s%d" % (name, r))
+            nc.scalar.activation(tile[:], g1[r][:].indirect(offsets[:]), COPY)
+            return tile
+
+        def subtract(r, plus):
+            g0[r] = sb.tile([P, J], F32, name="g0_%d" % r)
+            nc.vector.tensor_tensor(g0[r][:], plus, minus[r][:], ALU.subtract)
+
+        def put_maxima(r):
+            top = sb.tile([P, RUNS], F32, name="top%d" % r)
+            nc.vector.tensor_reduce(
+                top[:], g0[r][:].rearrange("p (n j) -> p n j", j=RUN), mybir.AxisListType.X, ALU.max
             )
-            nc.sync.dma_start(words_v[:, cols], y_codes[:].bitcast(I32))
+            nc.scalar.activation(put[r][:].indirect(put_list[:]), top[:], COPY)
+
+        for r in range(2):
+            for g in range(3):
+                product(r, g, g > 0)
+        product(2, 0, False)
+        product(2, 1, True)
+
+        minus[0] = look_up(0, "minus", minus_list)
+        minus[1] = look_up(1, "minus", minus_list)
+        product(3, 0, False)
+        product(3, 1, False)
+        subtract(0, g1[0][:].indirect(plus_list[:]))
+        product(2, 2, True)
+        put_maxima(0)
+        minus[2] = look_up(2, "minus", minus_list)
+        subtract(1, g1[1][:].indirect(plus_list[:]))
+        product(3, 2, True)
+        minus[3] = look_up(3, "minus", minus_list)
+        plus_last = look_up(3, "plus", plus_list)
+        put_maxima(1)
+        subtract(2, g1[2][:].indirect(plus_list[:]))
+        add_old(0, whole)
+        store(0)
+        put_maxima(2)
+        subtract(3, plus_last[:])
+        add_old(1, left)
+        put_maxima(3)
+        add_old(1, right)
+        store(1)
+        add_old(2, whole)
+        store(2)
+
+        pieces = [left, slice(half, half + P), slice(half + P, M)]
+        for cols in pieces:
+            add_old(3, cols)
+        store(3)
+
+        y_scales = sb.tile([P, M], U8, name="y_scales", align_bytes=64)
+        y_codes = [
+            sb.tile([P, half], U32, name="y_codes%d" % h, align_bytes=64) for h in range(2)
+        ]
+        words_v = out_1[0].rearrange("p m t -> p (m t)").bitcast(I32)
+        y_woven = []
+        for k, cols in enumerate(pieces):
+            width = cols.stop - cols.start
+            tile = sb.tile([P, width, PACK], BF16, name="y_woven%d" % k, align_bytes=64)
+            move(
+                k > 0,
+                tile[:].rearrange("p (g i) r -> p g r i", i=4),
+                y[:, :, cols].rearrange("p r (g i) -> p g r i", i=4),
+            )
+            y_woven.append(tile)
+
+        def quantise_result(k):
+            cols = pieces[k]
+            h, col = divmod(cols.start, half)
+            nc.vector.quantize_mx(
+                out=y_codes[h][:, col : col + cols.stop - cols.start].bitcast(FP8X4),
+                scales=y_scales[:, cols],
+                in_=y_woven[k][:].rearrange("p m r -> p (m r)"),
+            )
+
+        for k in range(1, len(pieces)):
+            quantise_result(k)
+        nc.sync.dma_start(words_v[:, right], y_codes[1][:].bitcast(I32))
+        quantise_result(0)
+        nc.sync.dma_start(words_v[:, left], y_codes[0][:].bitcast(I32))
         for q in range(4):
-            queue = nc.sync if q % 2 == 0 else nc.scalar
+            queue = nc.sync if q == 0 else nc.scalar
             queue.dma_start(
                 out_2[0, 4 * q : 4 * q + 4, :].bitcast(I32),
                 y_scales[32 * q : 32 * q + 4, :].bitcast(I32),

@@ -19,9 +19,14 @@ ALU = mybir.AluOpType
 
 P = 128
 PACK = 4
-BANK = 512
+LAST = PACK - 1
+QUADRANTS = 4
+
 WIDTHS = [256, 256, 128, 256, 128]
+FIRST_VECTOR_CHUNK = 3
+LOADS = [(0,), (1,), (2, 3), (4,)]
 STARTS = [sum(WIDTHS[:c]) for c in range(len(WIDTHS))]
+GROUPS = [((0, 1), "a"), ((2, 3), "b"), ((4,), "a")]
 
 
 def tile_attend_tab_looked_runsput_pl_kernel(
@@ -44,13 +49,16 @@ def tile_attend_tab_looked_runsput_pl_kernel(
         nc.sync.dma_start(key_list[:], offs)
 
         notes_v = notes.rearrange("(p t) u -> p t u", t=PACK)
-        raw = []
-        for c, width in enumerate(WIDTHS):
-            tile = sb.tile([P, PACK, width], F32, name="raw%d" % c)
-            nc.sync.dma_start(tile[:], notes_v[:, :, STARTS[c] : STARTS[c] + width])
-            raw.append(tile)
-            if c == 0:
-                for q in range(4):
+        raw = {}
+        for load, chunks in enumerate(LOADS):
+            start = STARTS[chunks[0]]
+            span = sum(WIDTHS[c] for c in chunks)
+            loaded = sb.tile([P, PACK, span], F32, name="raw%d" % load)
+            nc.sync.dma_start(loaded[:], notes_v[:, :, start : start + span])
+            for c in chunks:
+                raw[c] = loaded[:, :, STARTS[c] - start : STARTS[c] - start + WIDTHS[c]]
+            if load == 0:
+                for q in range(QUADRANTS):
                     nc.sync.dma_start(
                         pool_scales[32 * q : 32 * q + 4, :].bitcast(I32),
                         keys_scales[0, 4 * q : 4 * q + 4, :].bitcast(I32),
@@ -63,10 +71,10 @@ def tile_attend_tab_looked_runsput_pl_kernel(
 
         put = []
         for r in range(PACK):
-            tile = sb.tile([P, M], F32, name="put%d" % r)
-            engine = nc.gpsimd if r < 2 else nc.vector
-            engine.memset(tile[:], 0.0)
-            put.append(tile)
+            window = sb.tile([P, M], F32, name="put%d" % r)
+            engine = nc.gpsimd if r < PACK // 2 else nc.vector
+            engine.memset(window[:], 0.0)
+            put.append(window)
 
         picked_words = sb.tile([P, I], U16, name="picked_words", align_bytes=64)
         key_words = sb.tile([P, 2 * I], U8, name="key_words", align_bytes=64)
@@ -87,16 +95,21 @@ def tile_attend_tab_looked_runsput_pl_kernel(
             else:
                 nc.scalar.copy(dst, src)
 
+        def weaving_views(woven_tile, source):
+            return (
+                woven_tile[:].rearrange("p (g i) t -> p g t i", i=4),
+                source.rearrange("p t (g i) -> p g t i", i=4),
+            )
+
         woven, note_codes, note_scales = {}, {}, {}
 
         def weave(c):
             woven[c] = sb.tile([P, WIDTHS[c], PACK], BF16, name="woven%d" % c, align_bytes=64)
-            dst = woven[c][:].rearrange("p (g i) t -> p g t i", i=4)
-            src = raw[c][:].rearrange("p t (g i) -> p g t i", i=4)
+            dst, src = weaving_views(woven[c], raw[c])
             if c == 0:
                 nc.scalar.activation(dst, src, COPY)
             else:
-                move(c >= 3, dst, src)
+                move(c >= FIRST_VECTOR_CHUNK, dst, src)
 
         def quantise(c):
             note_codes[c] = sb.tile([P, WIDTHS[c]], U32, name="codes%d" % c, align_bytes=64)
@@ -113,15 +126,14 @@ def tile_attend_tab_looked_runsput_pl_kernel(
             quantise(c - 1)
         quantise(len(WIDTHS) - 1)
 
-        groups = [((0, 1), "a"), ((2, 3), "b"), ((4,), "a")]
         g1 = [sb.tile([P, U], F32, name="g1_%d" % r) for r in range(PACK)]
 
         def product(r, g, on_vector):
-            chunks, tag = groups[g]
+            chunks, letter = GROUPS[g]
             start = STARTS[chunks[0]]
             span = sum(WIDTHS[c] for c in chunks)
-            owner = 0 if (r, g) == (PACK - 1, 0) else r
-            bank = ps.tile([P, span], F32, name="bank", tag="%s%d" % (tag, owner))
+            owner = 0 if (r, g) == (LAST, 0) else r
+            bank = ps.tile([P, span], F32, name="bank", tag="%s%d" % (letter, owner))
             for c in chunks:
                 col = STARTS[c] - start
                 nc.tensor.matmul_mx(
@@ -138,6 +150,7 @@ def tile_attend_tab_looked_runsput_pl_kernel(
         y = sb.tile([P, PACK, M], F32, name="y")
         out_v = out_0.rearrange("(p r) m -> p r m", r=PACK)
         half = M // 2
+        whole, left, right = slice(0, M), slice(0, half), slice(half, M)
 
         def add_old(r, cols):
             nc.vector.tensor_tensor(y[:, r, cols], old_sb[:, r, cols], put[r][:, cols], ALU.add)
@@ -145,14 +158,12 @@ def tile_attend_tab_looked_runsput_pl_kernel(
         def store(r):
             nc.sync.dma_start(out_v[:, r, :], y[:, r, :])
 
-        whole, left, right = slice(0, M), slice(0, half), slice(half, M)
-
         minus, g0 = {}, {}
 
         def look_up(r, name, offsets):
-            tile = sb.tile([P, J], F32, name="%s%d" % (name, r))
-            nc.scalar.activation(tile[:], g1[r][:].indirect(offsets[:]), COPY)
-            return tile
+            looked = sb.tile([P, J], F32, name="%s%d" % (name, r))
+            nc.scalar.activation(looked[:], g1[r][:].indirect(offsets[:]), COPY)
+            return looked
 
         def subtract(r, plus):
             g0[r] = sb.tile([P, J], F32, name="g0_%d" % r)
@@ -166,31 +177,35 @@ def tile_attend_tab_looked_runsput_pl_kernel(
             nc.scalar.activation(put[r][:].indirect(put_list[:]), top[:], COPY)
 
         for r in range(2):
-            for g in range(3):
-                product(r, g, g > 0)
-        product(2, 0, False)
-        product(2, 1, True)
+            for g in range(len(GROUPS)):
+                product(r, g, on_vector=g > 0)
+        product(2, 0, on_vector=False)
+        product(2, 1, on_vector=True)
 
         minus[0] = look_up(0, "minus", minus_list)
         minus[1] = look_up(1, "minus", minus_list)
-        product(3, 0, False)
-        product(3, 1, False)
+        product(LAST, 0, on_vector=False)
+        product(LAST, 1, on_vector=False)
         subtract(0, g1[0][:].indirect(plus_list[:]))
-        product(2, 2, True)
+        product(2, 2, on_vector=True)
         put_maxima(0)
+
         minus[2] = look_up(2, "minus", minus_list)
         subtract(1, g1[1][:].indirect(plus_list[:]))
-        product(3, 2, True)
-        minus[3] = look_up(3, "minus", minus_list)
-        plus_last = look_up(3, "plus", plus_list)
+        product(LAST, 2, on_vector=True)
+        minus[LAST] = look_up(LAST, "minus", minus_list)
+        plus_last = look_up(LAST, "plus", plus_list)
         put_maxima(1)
+
         subtract(2, g1[2][:].indirect(plus_list[:]))
         add_old(0, whole)
         store(0)
         put_maxima(2)
-        subtract(3, plus_last[:])
+
+        subtract(LAST, plus_last[:])
         add_old(1, left)
-        put_maxima(3)
+        put_maxima(LAST)
+
         add_old(1, right)
         store(1)
         add_old(2, whole)
@@ -198,8 +213,8 @@ def tile_attend_tab_looked_runsput_pl_kernel(
 
         pieces = [left, slice(half, half + P), slice(half + P, M)]
         for cols in pieces:
-            add_old(3, cols)
-        store(3)
+            add_old(LAST, cols)
+        store(LAST)
 
         y_scales = sb.tile([P, M], U8, name="y_scales", align_bytes=64)
         y_codes = [
@@ -209,13 +224,9 @@ def tile_attend_tab_looked_runsput_pl_kernel(
         y_woven = []
         for k, cols in enumerate(pieces):
             width = cols.stop - cols.start
-            tile = sb.tile([P, width, PACK], BF16, name="y_woven%d" % k, align_bytes=64)
-            move(
-                k > 0,
-                tile[:].rearrange("p (g i) r -> p g r i", i=4),
-                y[:, :, cols].rearrange("p r (g i) -> p g r i", i=4),
-            )
-            y_woven.append(tile)
+            piece = sb.tile([P, width, PACK], BF16, name="y_woven%d" % k, align_bytes=64)
+            move(k > 0, *weaving_views(piece, y[:, :, cols]))
+            y_woven.append(piece)
 
         def quantise_result(k):
             cols = pieces[k]
@@ -231,7 +242,7 @@ def tile_attend_tab_looked_runsput_pl_kernel(
         nc.sync.dma_start(words_v[:, right], y_codes[1][:].bitcast(I32))
         quantise_result(0)
         nc.sync.dma_start(words_v[:, left], y_codes[0][:].bitcast(I32))
-        for q in range(4):
+        for q in range(QUADRANTS):
             queue = nc.sync if q == 0 else nc.scalar
             queue.dma_start(
                 out_2[0, 4 * q : 4 * q + 4, :].bitcast(I32),

from contextlib import ExitStack

import concourse.mybir as mybir

D, T, I, J, U, M, RUNS = 512, 2048, 512, 512, 1024, 512, 64
RUN = J // RUNS
FLOPS = 2 * D * I * U

F32 = mybir.dt.float32
BF16 = mybir.dt.bfloat16
I32 = mybir.dt.int32
U32 = mybir.dt.uint32
U16 = mybir.dt.uint16
U8 = mybir.dt.uint8
FP8X4 = mybir.dt.float8_e4m3fn_x4
FP4X4 = mybir.dt.float4_e2m1fn_x4
COPY = mybir.ActivationFunctionType.Copy
ALU = mybir.AluOpType

P = 128
PACK = 4
LAST = PACK - 1
QUADRANTS = 4

WIDTHS = [256, 256, 128, 256, 128]
FIRST_VECTOR_CHUNK = 3
LOADS = [(0,), (1,), (2, 3), (4,)]
STARTS = [sum(WIDTHS[:c]) for c in range(len(WIDTHS))]
GROUPS = [((0, 1), "a"), ((2, 3), "b"), ((4,), "a")]


def tile_attend_tab_looked_runsput_pl_kernel(
    tc, keys_words, keys_scales, notes, old, offs, offs2, offs3, offs4, out_0, out_1, out_2
):
    nc = tc.nc
    with ExitStack() as ctx:
        sb = ctx.enter_context(tc.tile_pool(name="sb", bufs=1))
        ps = ctx.enter_context(tc.psum_pool(name="ps", bufs=1))

        key_list = sb.tile([P, I // 16], U16, name="key_list")
        plus_list = sb.tile([P, J // 16], U16, name="plus_list")
        minus_list = sb.tile([P, J // 16], U16, name="minus_list")
        put_list = sb.tile([P, RUNS // 16], U16, name="put_list")

        pool_words = sb.tile([P, T], U16, name="pool_words", align_bytes=64)
        pool_scales = sb.tile([P, T], U8, name="pool_scales", align_bytes=64)
        nc.gpsimd.memset(pool_scales[:].bitcast(I32), 0)
        nc.sync.dma_start(pool_words[:].bitcast(I32), keys_words[0].bitcast(I32))
        nc.sync.dma_start(key_list[:], offs)

        notes_v = notes.rearrange("(p t) u -> p t u", t=PACK)
        raw = {}
        for load, chunks in enumerate(LOADS):
            start = STARTS[chunks[0]]
            span = sum(WIDTHS[c] for c in chunks)
            loaded = sb.tile([P, PACK, span], F32, name="raw%d" % load)
            nc.sync.dma_start(loaded[:], notes_v[:, :, start : start + span])
            for c in chunks:
                raw[c] = loaded[:, :, STARTS[c] - start : STARTS[c] - start + WIDTHS[c]]
            if load == 0:
                for q in range(QUADRANTS):
                    nc.sync.dma_start(
                        pool_scales[32 * q : 32 * q + 4, :].bitcast(I32),
                        keys_scales[0, 4 * q : 4 * q + 4, :].bitcast(I32),
                    )
        nc.sync.dma_start(minus_list[:], offs3)
        nc.sync.dma_start(plus_list[:], offs2)
        nc.sync.dma_start(put_list[:], offs4)
        old_sb = sb.tile([P, PACK, M], F32, name="old_sb")
        nc.sync.dma_start(old_sb[:], old.rearrange("(p r) m -> p r m", r=PACK))

        put = []
        for r in range(PACK):
            window = sb.tile([P, M], F32, name="put%d" % r)
            engine = nc.gpsimd if r < PACK // 2 else nc.vector
            engine.memset(window[:], 0.0)
            put.append(window)

        picked_words = sb.tile([P, I], U16, name="picked_words", align_bytes=64)
        key_words = sb.tile([P, 2 * I], U8, name="key_words", align_bytes=64)
        key_scales = sb.tile([P, I], U8, name="key_scales", align_bytes=64)
        nc.vector.tensor_copy(picked_words[:], pool_words[:].indirect(key_list[:]))
        nc.vector.tensor_copy(
            key_words[:].bitcast(U16).rearrange("p (r s) -> p r s", r=PACK),
            picked_words[:].rearrange("p (s r) -> p r s", r=PACK),
        )
        nc.vector.tensor_copy(
            key_scales[:].rearrange("p (r s) -> p s r", r=PACK),
            pool_scales[:].indirect(key_list[:]),
        )

        def move(on_vector, dst, src):
            if on_vector:
                nc.vector.tensor_copy(dst, src)
            else:
                nc.scalar.copy(dst, src)

        def weaving_views(woven_tile, source):
            return (
                woven_tile[:].rearrange("p (g i) t -> p g t i", i=4),
                source.rearrange("p t (g i) -> p g t i", i=4),
            )

        woven, note_codes, note_scales = {}, {}, {}

        def weave(c):
            woven[c] = sb.tile([P, WIDTHS[c], PACK], BF16, name="woven%d" % c, align_bytes=64)
            dst, src = weaving_views(woven[c], raw[c])
            if c == 0:
                nc.scalar.activation(dst, src, COPY)
            else:
                move(c >= FIRST_VECTOR_CHUNK, dst, src)

        def quantise(c):
            note_codes[c] = sb.tile([P, WIDTHS[c]], U32, name="codes%d" % c, align_bytes=64)
            note_scales[c] = sb.tile([P, WIDTHS[c]], U8, name="scales%d" % c, align_bytes=64)
            nc.vector.quantize_mx(
                out=note_codes[c][:].bitcast(FP8X4),
                scales=note_scales[c][:],
                in_=woven[c][:].rearrange("p u t -> p (u t)"),
            )

        weave(0)
        for c in range(1, len(WIDTHS)):
            weave(c)
            quantise(c - 1)
        quantise(len(WIDTHS) - 1)

        g1 = [sb.tile([P, U], F32, name="g1_%d" % r) for r in range(PACK)]

        def product(r, g, on_vector):
            chunks, letter = GROUPS[g]
            start = STARTS[chunks[0]]
            span = sum(WIDTHS[c] for c in chunks)
            owner = 0 if (r, g) == (LAST, 0) else r
            bank = ps.tile([P, span], F32, name="bank", tag="%s%d" % (letter, owner))
            for c in chunks:
                col = STARTS[c] - start
                nc.tensor.matmul_mx(
                    out=bank[:, col : col + WIDTHS[c]],
                    lhsT=key_words[:, 2 * P * r : 2 * P * (r + 1)].bitcast(FP4X4),
                    lhsT_scale=key_scales[:, P * r : P * (r + 1)],
                    rhs=note_codes[c][:].bitcast(FP8X4),
                    rhs_scale=note_scales[c][:],
                    start=True,
                    stop=True,
                )
            move(on_vector, g1[r][:, start : start + span], bank[:])

        y = sb.tile([P, PACK, M], F32, name="y")
        out_v = out_0.rearrange("(p r) m -> p r m", r=PACK)
        half = M // 2
        whole, left, right = slice(0, M), slice(0, half), slice(half, M)

        def add_old(r, cols):
            nc.vector.tensor_tensor(y[:, r, cols], old_sb[:, r, cols], put[r][:, cols], ALU.add)

        def store(r):
            nc.sync.dma_start(out_v[:, r, :], y[:, r, :])

        minus, g0 = {}, {}

        def look_up(r, name, offsets):
            looked = sb.tile([P, J], F32, name="%s%d" % (name, r))
            nc.scalar.activation(looked[:], g1[r][:].indirect(offsets[:]), COPY)
            return looked

        def subtract(r, plus):
            g0[r] = sb.tile([P, J], F32, name="g0_%d" % r)
            nc.vector.tensor_tensor(g0[r][:], plus, minus[r][:], ALU.subtract)

        def put_maxima(r):
            top = sb.tile([P, RUNS], F32, name="top%d" % r)
            nc.vector.tensor_reduce(
                top[:], g0[r][:].rearrange("p (n j) -> p n j", j=RUN), mybir.AxisListType.X, ALU.max
            )
            nc.scalar.activation(put[r][:].indirect(put_list[:]), top[:], COPY)

        for r in range(2):
            for g in range(len(GROUPS)):
                product(r, g, on_vector=g > 0)
        product(2, 0, on_vector=False)
        product(2, 1, on_vector=True)

        minus[0] = look_up(0, "minus", minus_list)
        minus[1] = look_up(1, "minus", minus_list)
        product(LAST, 0, on_vector=False)
        product(LAST, 1, on_vector=False)
        subtract(0, g1[0][:].indirect(plus_list[:]))
        product(2, 2, on_vector=True)
        put_maxima(0)

        minus[2] = look_up(2, "minus", minus_list)
        subtract(1, g1[1][:].indirect(plus_list[:]))
        product(LAST, 2, on_vector=True)
        minus[LAST] = look_up(LAST, "minus", minus_list)
        plus_last = look_up(LAST, "plus", plus_list)
        put_maxima(1)

        subtract(2, g1[2][:].indirect(plus_list[:]))
        add_old(0, whole)
        store(0)
        put_maxima(2)

        subtract(LAST, plus_last[:])
        add_old(1, left)
        put_maxima(LAST)

        add_old(1, right)
        store(1)
        add_old(2, whole)
        store(2)

        pieces = [left, slice(half, half + P), slice(half + P, M)]
        for cols in pieces:
            add_old(LAST, cols)
        store(LAST)

        y_scales = sb.tile([P, M], U8, name="y_scales", align_bytes=64)
        y_codes = [
            sb.tile([P, half], U32, name="y_codes%d" % h, align_bytes=64) for h in range(2)
        ]
        words_v = out_1[0].rearrange("p m t -> p (m t)").bitcast(I32)
        y_woven = []
        for k, cols in enumerate(pieces):
            width = cols.stop - cols.start
            piece = sb.tile([P, width, PACK], BF16, name="y_woven%d" % k, align_bytes=64)
            move(k > 0, *weaving_views(piece, y[:, :, cols]))
            y_woven.append(piece)

        def quantise_result(k):
            cols = pieces[k]
            h, col = divmod(cols.start, half)
            nc.vector.quantize_mx(
                out=y_codes[h][:, col : col + cols.stop - cols.start].bitcast(FP8X4),
                scales=y_scales[:, cols],
                in_=y_woven[k][:].rearrange("p m r -> p (m r)"),
            )

        for k in range(1, len(pieces)):
            quantise_result(k)
        nc.sync.dma_start(words_v[:, right], y_codes[1][:].bitcast(I32))
        quantise_result(0)
        nc.sync.dma_start(words_v[:, left], y_codes[0][:].bitcast(I32))
        for q in range(QUADRANTS):
            queue = nc.sync if q == 0 else nc.scalar
            queue.dma_start(
                out_2[0, 4 * q : 4 * q + 4, :].bitcast(I32),
                y_scales[32 * q : 32 * q + 4, :].bitcast(I32),
            )
